import numpy as np
import ml_dtypes


def mxq(x, axis, fmt="e4m3"):
    dtype, down = {"e4m3": (ml_dtypes.float8_e4m3fn, 7), "e5m2": (ml_dtypes.float8_e5m2, 14)}[fmt]
    v = np.moveaxis(np.asarray(x, np.float32).astype(ml_dtypes.bfloat16).astype(np.float64), axis, -1)
    blocks = v.reshape(v.shape[:-1] + (-1, 32))
    amax = np.abs(blocks).max(-1, keepdims=True)
    byte = np.maximum(np.where(amax > 0, np.frexp(amax)[1] - 1 + 127, 0) - down, 1)
    scale = np.exp2(byte - 127.0)
    codes = (blocks / scale).astype(np.float32).astype(dtype).astype(np.float64)
    return np.moveaxis((codes * scale).reshape(v.shape), -1, axis)


WIDE = False


def mx_kscale(k):
    if not WIDE:
        return np.ones(k)
    levels = np.array([10, -10, 5, -5, 0])
    if k % 512:
        return np.exp2(np.random.permutation(np.resize(levels, k // 32))).repeat(32)
    a = np.empty((k // 512, 16))
    for p in range(k // 512):
        a[p, :8] = np.random.permutation(np.resize(levels, 8))
        for g in range(8):
            far = levels[np.abs(levels - a[p, g]) >= 10]
            a[p, g + 8] = far[np.random.randint(len(far))]
    return np.exp2(a.ravel()).repeat(32)


def f64(x):
    return np.asarray(x).astype(np.float64)


def striped(idx):
    return np.tile(idx.reshape(-1, 16).T, (8, 1)).astype(np.uint16)


def unstriped(offs):
    return offs[:16].T.reshape(-1).astype(np.int64)


def sigmoid(v):
    return 1.0 / (1.0 + np.exp(-np.maximum(v, -700.0)))


K, T, E, C, H, N = 2048, 640, 2, 256, 512, 512


def by_expert(wq, xq):
    return np.concatenate([wq[e].T @ xq[:, e * C:(e + 1) * C] for e in range(E)], axis=1)


def setup_inputs():
    n = np.random.standard_normal
    s = mx_kscale(K)[:, None]
    u = mx_kscale(H)
    return {
        "xT": (n((K, T)) * s).astype(np.float32),
        "xr": n((N, T)).astype(np.float32),
        "w1": (n((E, K, H)) / np.sqrt(K) / s[None]).astype(np.float32),
        "w3": (n((E, K, H)) / np.sqrt(K) / s[None] * u[None, None, :]).astype(np.float32),
        "w2": (n((E, H, N)) / np.sqrt(H) / u[None, :, None]).astype(np.float32),
        "gate": np.tile(np.random.uniform(0.2, 1.0, E * C), (N, 1)).astype(np.float32),
        "offs": striped(np.random.permutation(T)[:E * C]),
    }


def reference(xT, xr, w1, w3, w2, gate, offs):
    idx = unstriped(offs)
    xq = mxq(f64(xT)[:, idx], 0, "e4m3")
    h = sigmoid(by_expert(mxq(f64(w1), 1, "e4m3"), xq))
    h = h * by_expert(mxq(f64(w3), 1, "e4m3"), xq)
    y = by_expert(mxq(f64(w2), 1, "e4m3"), mxq(h, 0, "e4m3"))
    out = f64(xr).copy()
    out[:, idx] += f64(gate) * y
    return out

@@ -1,0 +1,218 @@
+from contextlib import ExitStack
+
+import concourse.mybir as mybir
+
+K, T, E, C, H, N = 2048, 640, 2, 256, 512, 512
+P = 128
+PACK = 4
+K_PASS = P * PACK
+PASSES = K // K_PASS
+
+F32 = mybir.dt.float32
+BF16 = mybir.dt.bfloat16
+U32 = mybir.dt.uint32
+I32 = mybir.dt.int32
+U16 = mybir.dt.uint16
+U8 = mybir.dt.uint8
+FP8X4 = mybir.dt.float8_e4m3fn_x4
+MULT, ADD = mybir.AluOpType.mult, mybir.AluOpType.add
+COPY = mybir.ActivationFunctionType.Copy
+SIGMOID = mybir.ActivationFunctionType.Sigmoid
+
+FLOPS = 2 * E * C * (2 * K * H + H * N)
+
+X_VECTOR = 56
+
+
+def vector_share(key):
+    if key[0] == "w2":
+        return 44 if key[1] == 0 else 0
+    e, m, s = key
+    if e == 0:
+        return 40
+    if m == "b" and s >= 2:
+        return 64
+    return 24
+
+
+def tile_moe_res_glu_sigmoid_kernel(tc, xT, xr, w1, w3, w2, gate, offs, out):
+    nc = tc.nc
+    with ExitStack() as ctx:
+        keep = ctx.enter_context(tc.tile_pool(name="keep", bufs=1))
+        stage = ctx.enter_context(tc.tile_pool(name="stage", bufs=11))
+        work = ctx.enter_context(tc.tile_pool(name="work", bufs=4))
+        coded = ctx.enter_context(tc.tile_pool(name="coded", bufs=12))
+        psum = ctx.enter_context(tc.psum_pool(name="psum", bufs=1))
+
+        offsets = keep.tile([P, E * C // 16], U16, name="offsets")
+        nc.sync.dma_start(offsets[:], offs)
+
+        warm = keep.tile([P, 8], F32, name="warm")
+        nc.gpsimd.memset(warm[:], 0.0)
+        warm_out = keep.tile([P, 8], F32, name="warm_out")
+        nc.scalar.activation(warm_out[:], warm[:], SIGMOID)
+
+        x_plane = keep.tile([P, T], U8, name="x_plane", align_bytes=64)
+        nc.gpsimd.memset(x_plane[:], 0)
+        windows = []
+        for q in range(4):
+            window = keep.tile([P, T], F32, name=f"window{q}")
+            nc.gpsimd.memset(window[:], 0.0)
+            windows.append(window)
+
+        x_words = [keep.tile([P, T], U32, name=f"x_words{s}", align_bytes=64) for s in range(PASSES)]
+        slot_words = [[keep.tile([P, C], U32, name=f"slot_words{e}_{s}", align_bytes=64) for s in range(PASSES)] for e in range(E)]
+        slot_planes = [keep.tile([P, C], U8, name=f"slot_plane{e}", align_bytes=64) for e in range(E)]
+        sums = {}
+        held = {}
+
+        def lists(e):
+            return offsets[:, e * (C // 16) : (e + 1) * (C // 16)]
+
+        def load(view, columns):
+            raw = stage.tile([P, PACK, columns], F32, name="raw", align_bytes=64)
+            nc.sync.dma_start(raw[:], view)
+            return raw
+
+        def x_copy(s):
+            raw = load(xT[s * K_PASS : (s + 1) * K_PASS, :].rearrange("(p j) t -> p j t", j=PACK), T)
+            grouped = work.tile([P, T * PACK], BF16, name="grouped", align_bytes=64)
+            src = raw[:].rearrange("p j (c i) -> p c j i", i=4)
+            dst = grouped[:].rearrange("p (c i j) -> p c j i", i=4, j=PACK)
+            nc.vector.tensor_copy(dst[:, :X_VECTOR], src[:, :X_VECTOR])
+            nc.scalar.activation(dst[:, X_VECTOR:], src[:, X_VECTOR:], COPY)
+            held["x", s] = grouped
+
+        def gather_words(e, s):
+            nc.vector.tensor_copy(slot_words[e][s][:], x_words[s][:].indirect(lists(e)))
+
+        def x_finish(s):
+            grouped = held["x", s]
+            for lo, hi in ((0, 512), (512, T)):
+                nc.vector.quantize_mx(
+                    out=x_words[s][:, lo:hi].bitcast(FP8X4),
+                    scales=x_plane[4 * s : P, lo:hi],
+                    in_=grouped[:, lo * PACK : hi * PACK],
+                )
+            gather_words(0, s)
+            if s == PASSES - 1:
+                nc.vector.tensor_copy(slot_planes[0][:], x_plane[:].indirect(lists(0)))
+
+        def w_copy(key, view):
+            raw = load(view.rearrange("(p j) c -> p j c", j=PACK), 512)
+            grouped = work.tile([P, 512 * PACK], BF16, name="grouped", align_bytes=64)
+            src = raw[:].rearrange("p j (m t) -> p m j t", t=4)
+            dst = grouped[:].rearrange("p (t m j) -> p m j t", t=4, j=PACK)
+            share = vector_share(key)
+            if share:
+                nc.vector.tensor_copy(dst[:, :share], src[:, :share])
+            nc.scalar.copy(dst[:, share:], src[:, share:])
+            held[key] = grouped
+
+        def w_quantize(key):
+            words = coded.tile([P, 512], U32, name="w_words", align_bytes=64)
+            plane = coded.tile([P, 512], U8, name="w_plane", align_bytes=64)
+            nc.vector.quantize_mx(out=words[:].bitcast(FP8X4), scales=plane[:], in_=held[key][:])
+            return words, plane
+
+        def first_layer(key):
+            e, m, s = key
+            words, plane = w_quantize(key)
+            for t in range(4):
+                if s == 0:
+                    sums[e, m, t] = psum.tile([P, 512], F32, name=f"bank_{m}_{t}")
+                cols = slice(t * P, (t + 1) * P)
+                nc.tensor.matmul_mx(
+                    out=sums[e, m, t][:, :C],
+                    lhsT=words[:, cols].bitcast(FP8X4),
+                    lhsT_scale=plane[:, cols],
+                    rhs=slot_words[e][s][:].bitcast(FP8X4),
+                    rhs_scale=slot_planes[e][4 * s : P, :],
+                    start=(s == 0),
+                    stop=(s == PASSES - 1),
+                )
+            if s < PASSES - 1:
+                return
+            if m == "a":
+                sig = work.tile([P, 4, C], F32, name="sig", bufs=1)
+                for t in range(4):
+                    nc.scalar.activation(sig[:, t, :], sums[e, m, t][:, :C], SIGMOID)
+                held["sig", e] = sig
+            else:
+                hidden = work.tile([P, 4, C], BF16, name="hidden", bufs=1)
+                for t in range(4):
+                    nc.vector.tensor_tensor(hidden[:, t, :], held["sig", e][:, t, :], sums[e, m, t][:, :C], MULT)
+                h_grouped = work.tile([P, C * PACK], BF16, name="h_grouped", bufs=1, align_bytes=64)
+                nc.vector.tensor_copy(
+                    h_grouped[:].rearrange("p (c i t) -> p c t i", i=4, t=4),
+                    hidden[:].rearrange("p t (c i) -> p c t i", i=4),
+                )
+                h_words = work.tile([P, C], U32, name="h_words", bufs=2, align_bytes=64)
+                h_plane = work.tile([P, C], U8, name="h_plane", bufs=2, align_bytes=64)
+                nc.vector.quantize_mx(out=h_words[:].bitcast(FP8X4), scales=h_plane[:], in_=h_grouped[:])
+                held["h", e] = h_words, h_plane
+
+        def second_layer(e, q):
+            words, plane = held["w2q", e]
+            h_words, h_plane = held["h", e]
+            m = "b" if e == 0 else "a"
+            bank = psum.tile([P, 512], F32, name=f"bank_{m}_{q}")
+            cols = slice(q * P, (q + 1) * P)
+            nc.tensor.matmul_mx(
+                out=bank[:, :C],
+                lhsT=words[:, cols].bitcast(FP8X4),
+                lhsT_scale=plane[:, cols],
+                rhs=h_words[:].bitcast(FP8X4),
+                rhs_scale=h_plane[:],
+                start=True,
+                stop=True,
+            )
+            y = work.tile([P, C], F32, name="y")
+            nc.scalar.copy(y[:], bank[:, :C])
+            nc.vector.tensor_tensor(windows[q][:].indirect(lists(e)), y[:], held["gate", e][:, q, :], MULT)
+
+        def rows(dram):
+            return dram.rearrange("(p q) t -> p q t", q=4)
+
+        plan = [("x", s) for s in range(PASSES)]
+        for e in range(E):
+            plan += [(e, "a", s) for s in range(PASSES)] + [(e, "b", s) for s in range(PASSES)] + [("w2", e)]
+
+        def copy_step(key):
+            if key[0] == "x":
+                x_copy(key[1])
+            elif key[0] == "w2":
+                e = key[1]
+                w_copy(key, w2[e])
+                held["gate", e] = load(rows(gate)[:, :, e * C : (e + 1) * C], C)
+            else:
+                e, m, s = key
+                w_copy(key, (w1 if m == "a" else w3)[e, s * K_PASS : (s + 1) * K_PASS, :])
+
+        def finish_step(key):
+            if key[0] == "x":
+                x_finish(key[1])
+            elif key[0] == "w2":
+                held["w2q", key[1]] = w_quantize(key)
+            else:
+                first_layer(key)
+                e, m, s = key
+                if e == 0 and m == "a":
+                    gather_words(1, s)
+                    if s == 0:
+                        nc.vector.tensor_copy(slot_planes[1][:], x_plane[:].indirect(lists(1)))
+                if e == 1 and m == "a":
+                    second_layer(0, s)
+
+        for i, key in enumerate(plan):
+            copy_step(key)
+            if i > 0:
+                finish_step(plan[i - 1])
+        finish_step(plan[-1])
+
+        residual = load(rows(xr), T)
+        for q in range(4):
+            second_layer(1, q)
+            result = work.tile([P, T], F32, name="result", bufs=2)
+            nc.vector.tensor_tensor(result[:], windows[q][:], residual[:, q, :], ADD)
+            nc.sync.dma_start(rows(out)[:, q, :], result[:])

@@ -21,18 +21,8 @@ SIGMOID = mybir.ActivationFunctionType.Sigmoid
 
 FLOPS = 2 * E * C * (2 * K * H + H * N)
 
-X_VECTOR = 56
-
-
-def vector_share(key):
-    if key[0] == "w2":
-        return 44 if key[1] == 0 else 0
-    e, m, s = key
-    if e == 0:
-        return 40
-    if m == "b" and s >= 2:
-        return 64
-    return 24
+X_VECTOR = 64
+W_VECTOR = 64
 
 
 def tile_moe_res_glu_sigmoid_kernel(tc, xT, xr, w1, w3, w2, gate, offs, out):
@@ -103,7 +93,7 @@ def tile_moe_res_glu_sigmoid_kernel(tc, xT, xr, w1, w3, w2, gate, offs, out):
             grouped = work.tile([P, 512 * PACK], BF16, name="grouped", align_bytes=64)
             src = raw[:].rearrange("p j (m t) -> p m j t", t=4)
             dst = grouped[:].rearrange("p (t m j) -> p m j t", t=4, j=PACK)
-            share = vector_share(key)
+            share = 0 if key == ("w2", 1) else W_VECTOR
             if share:
                 nc.vector.tensor_copy(dst[:, :share], src[:, :share])
             nc.scalar.copy(dst[:, share:], src[:, share:])

@@ -21,8 +21,18 @@ SIGMOID = mybir.ActivationFunctionType.Sigmoid
 
 FLOPS = 2 * E * C * (2 * K * H + H * N)
 
-X_VECTOR = 64
-W_VECTOR = 64
+WINDOW = 704
+X_VECTOR = 40
+
+
+def vector_share(key):
+    if key == ("w2", 1):
+        return 0
+    if key in ((1, "b", 2), (1, "b", 3)):
+        return 56
+    if key in ((1, "b", 0), (1, "b", 1)):
+        return 40
+    return 32
 
 
 def tile_moe_res_glu_sigmoid_kernel(tc, xT, xr, w1, w3, w2, gate, offs, out):
@@ -35,24 +45,27 @@ def tile_moe_res_glu_sigmoid_kernel(tc, xT, xr, w1, w3, w2, gate, offs, out):
         psum = ctx.enter_context(tc.psum_pool(name="psum", bufs=1))
 
         offsets = keep.tile([P, E * C // 16], U16, name="offsets")
-        nc.sync.dma_start(offsets[:], offs)
 
         warm = keep.tile([P, 8], F32, name="warm")
         nc.gpsimd.memset(warm[:], 0.0)
         warm_out = keep.tile([P, 8], F32, name="warm_out")
         nc.scalar.activation(warm_out[:], warm[:], SIGMOID)
 
-        x_plane = keep.tile([P, T], U8, name="x_plane", align_bytes=64)
+        x_plane = keep.tile([P, WINDOW], U8, name="x_plane", align_bytes=64)
         nc.gpsimd.memset(x_plane[:], 0)
+        x_words = []
+        for s in range(PASSES):
+            words = keep.tile([P, WINDOW], I32, name=f"x_words{s}", align_bytes=64)
+            nc.gpsimd.memset(words[:, T:], 0)
+            x_words.append(words)
         windows = []
         for q in range(4):
             window = keep.tile([P, T], F32, name=f"window{q}")
             nc.gpsimd.memset(window[:], 0.0)
             windows.append(window)
 
-        x_words = [keep.tile([P, T], U32, name=f"x_words{s}", align_bytes=64) for s in range(PASSES)]
-        slot_words = [[keep.tile([P, C], U32, name=f"slot_words{e}_{s}", align_bytes=64) for s in range(PASSES)] for e in range(E)]
-        slot_planes = [keep.tile([P, C], U8, name=f"slot_plane{e}", align_bytes=64) for e in range(E)]
+        slot_words = [keep.tile([P, E * C], U32, name=f"slot_words{s}", align_bytes=64) for s in range(PASSES)]
+        slot_plane = keep.tile([P, E * C], U8, name="slot_plane", align_bytes=64)
         sums = {}
         held = {}
 
@@ -66,15 +79,14 @@ def tile_moe_res_glu_sigmoid_kernel(tc, xT, xr, w1, w3, w2, gate, offs, out):
 
         def x_copy(s):
             raw = load(xT[s * K_PASS : (s + 1) * K_PASS, :].rearrange("(p j) t -> p j t", j=PACK), T)
-            grouped = work.tile([P, T * PACK], BF16, name="grouped", align_bytes=64)
+            grouped = work.tile([P, T * PACK], BF16, name="grouped", bufs=6, align_bytes=64)
             src = raw[:].rearrange("p j (c i) -> p c j i", i=4)
             dst = grouped[:].rearrange("p (c i j) -> p c j i", i=4, j=PACK)
             nc.vector.tensor_copy(dst[:, :X_VECTOR], src[:, :X_VECTOR])
             nc.scalar.activation(dst[:, X_VECTOR:], src[:, X_VECTOR:], COPY)
             held["x", s] = grouped
-
-        def gather_words(e, s):
-            nc.vector.tensor_copy(slot_words[e][s][:], x_words[s][:].indirect(lists(e)))
+            if s == 0:
+                nc.sync.dma_start(offsets[:], offs)
 
         def x_finish(s):
             grouped = held["x", s]
@@ -84,16 +96,16 @@ def tile_moe_res_glu_sigmoid_kernel(tc, xT, xr, w1, w3, w2, gate, offs, out):
                     scales=x_plane[4 * s : P, lo:hi],
                     in_=grouped[:, lo * PACK : hi * PACK],
                 )
-            gather_words(0, s)
+            nc.vector.tensor_copy(slot_words[s][:], x_words[s][:].bitcast(U32).indirect(offsets[:]))
             if s == PASSES - 1:
-                nc.vector.tensor_copy(slot_planes[0][:], x_plane[:].indirect(lists(0)))
+                nc.vector.tensor_copy(slot_plane[:], x_plane[:].indirect(offsets[:]))
 
         def w_copy(key, view):
             raw = load(view.rearrange("(p j) c -> p j c", j=PACK), 512)
-            grouped = work.tile([P, 512 * PACK], BF16, name="grouped", align_bytes=64)
+            grouped = work.tile([P, 512 * PACK], BF16, name="grouped", bufs=6, align_bytes=64)
             src = raw[:].rearrange("p j (m t) -> p m j t", t=4)
             dst = grouped[:].rearrange("p (t m j) -> p m j t", t=4, j=PACK)
-            share = 0 if key == ("w2", 1) else W_VECTOR
+            share = vector_share(key)
             if share:
                 nc.vector.tensor_copy(dst[:, :share], src[:, :share])
             nc.scalar.copy(dst[:, share:], src[:, share:])
@@ -116,8 +128,8 @@ def tile_moe_res_glu_sigmoid_kernel(tc, xT, xr, w1, w3, w2, gate, offs, out):
                     out=sums[e, m, t][:, :C],
                     lhsT=words[:, cols].bitcast(FP8X4),
                     lhsT_scale=plane[:, cols],
-                    rhs=slot_words[e][s][:].bitcast(FP8X4),
-                    rhs_scale=slot_planes[e][4 * s : P, :],
+                    rhs=slot_words[s][:, e * C : (e + 1) * C].bitcast(FP8X4),
+                    rhs_scale=slot_plane[4 * s : P, e * C : (e + 1) * C],
                     start=(s == 0),
                     stop=(s == PASSES - 1),
                 )
@@ -142,14 +154,12 @@ def tile_moe_res_glu_sigmoid_kernel(tc, xT, xr, w1, w3, w2, gate, offs, out):
                 nc.vector.quantize_mx(out=h_words[:].bitcast(FP8X4), scales=h_plane[:], in_=h_grouped[:])
                 held["h", e] = h_words, h_plane
 
-        def second_layer(e, q):
+        def second_layer(e, q, bank, half):
             words, plane = held["w2q", e]
             h_words, h_plane = held["h", e]
-            m = "b" if e == 0 else "a"
-            bank = psum.tile([P, 512], F32, name=f"bank_{m}_{q}")
             cols = slice(q * P, (q + 1) * P)
             nc.tensor.matmul_mx(
-                out=bank[:, :C],
+                out=bank[:, half * C : (half + 1) * C],
                 lhsT=words[:, cols].bitcast(FP8X4),
                 lhsT_scale=plane[:, cols],
                 rhs=h_words[:].bitcast(FP8X4),
@@ -157,9 +167,17 @@ def tile_moe_res_glu_sigmoid_kernel(tc, xT, xr, w1, w3, w2, gate, offs, out):
                 start=True,
                 stop=True,
             )
-            y = work.tile([P, C], F32, name="y")
-            nc.scalar.copy(y[:], bank[:, :C])
-            nc.vector.tensor_tensor(windows[q][:].indirect(lists(e)), y[:], held["gate", e][:, q, :], MULT)
+
+        def pair(e, u):
+            bank = psum.tile([P, 512], F32, name=f"bank_b_{u}")
+            for half in range(2):
+                second_layer(e, 2 * u + half, bank, half)
+            y = work.tile([P, 2, C], F32, name="y", bufs=2)
+            nc.scalar.copy(y[:].rearrange("p a c -> p (a c)"), bank[:])
+            held["y", u] = y
+
+        def scatter(e, q):
+            nc.vector.tensor_tensor(windows[q][:].indirect(lists(e)), held["y", q // 2][:, q % 2, :], held["gate", e][:, q, :], MULT)
 
         def rows(dram):
             return dram.rearrange("(p q) t -> p q t", q=4)
@@ -187,12 +205,12 @@ def tile_moe_res_glu_sigmoid_kernel(tc, xT, xr, w1, w3, w2, gate, offs, out):
             else:
                 first_layer(key)
                 e, m, s = key
-                if e == 0 and m == "a":
-                    gather_words(1, s)
-                    if s == 0:
-                        nc.vector.tensor_copy(slot_planes[1][:], x_plane[:].indirect(lists(1)))
-                if e == 1 and m == "a":
-                    second_layer(0, s)
+                if e == 1:
+                    i = s if m == "a" else 4 + s
+                    if i < 2:
+                        pair(0, i)
+                    if i in (1, 3, 5, 7):
+                        scatter(0, i // 2)
 
         for i, key in enumerate(plan):
             copy_step(key)
@@ -201,8 +219,21 @@ def tile_moe_res_glu_sigmoid_kernel(tc, xT, xr, w1, w3, w2, gate, offs, out):
         finish_step(plan[-1])
 
         residual = load(rows(xr), T)
-        for q in range(4):
-            second_layer(1, q)
-            result = work.tile([P, T], F32, name="result", bufs=2)
-            nc.vector.tensor_tensor(result[:], windows[q][:], residual[:, q, :], ADD)
+        scaled = []
+
+        def finish(q):
+            nc.vector.tensor_copy(windows[q][:].indirect(lists(1)), scaled[q][:])
+            result = work.tile([P, T], F32, name="result")
+            engine = nc.gpsimd if q < 3 else nc.vector
+            engine.tensor_tensor(result[:], windows[q][:], residual[:, q, :], ADD)
             nc.sync.dma_start(rows(out)[:, q, :], result[:])
+
+        for q in range(4):
+            bank = psum.tile([P, 512], F32, name=f"bank_a_{q}")
+            second_layer(1, q, bank, 0)
+            z = work.tile([P, C], F32, name="z")
+            nc.vector.tensor_tensor(z[:], bank[:, :C], held["gate", 1][:, q, :], MULT)
+            scaled.append(z)
+            if q > 0:
+                finish(q - 1)
+        finish(3)

from contextlib import ExitStack

import concourse.mybir as mybir

K, T, E, C, H, N = 2048, 640, 2, 256, 512, 512
P = 128
PACK = 4
K_PASS = P * PACK
PASSES = K // K_PASS

F32 = mybir.dt.float32
BF16 = mybir.dt.bfloat16
U32 = mybir.dt.uint32
I32 = mybir.dt.int32
U16 = mybir.dt.uint16
U8 = mybir.dt.uint8
FP8X4 = mybir.dt.float8_e4m3fn_x4
MULT, ADD = mybir.AluOpType.mult, mybir.AluOpType.add
COPY = mybir.ActivationFunctionType.Copy
SIGMOID = mybir.ActivationFunctionType.Sigmoid

FLOPS = 2 * E * C * (2 * K * H + H * N)

WINDOW = 704
X_VECTOR = 40


def vector_share(key):
    if key == ("w2", 1):
        return 0
    if key in ((1, "b", 2), (1, "b", 3)):
        return 56
    if key in ((1, "b", 0), (1, "b", 1)):
        return 40
    return 32


def tile_moe_res_glu_sigmoid_kernel(tc, xT, xr, w1, w3, w2, gate, offs, out):
    nc = tc.nc
    with ExitStack() as ctx:
        keep = ctx.enter_context(tc.tile_pool(name="keep", bufs=1))
        stage = ctx.enter_context(tc.tile_pool(name="stage", bufs=11))
        work = ctx.enter_context(tc.tile_pool(name="work", bufs=4))
        coded = ctx.enter_context(tc.tile_pool(name="coded", bufs=12))
        psum = ctx.enter_context(tc.psum_pool(name="psum", bufs=1))

        offsets = keep.tile([P, E * C // 16], U16, name="offsets")

        warm = keep.tile([P, 8], F32, name="warm")
        nc.gpsimd.memset(warm[:], 0.0)
        warm_out = keep.tile([P, 8], F32, name="warm_out")
        nc.scalar.activation(warm_out[:], warm[:], SIGMOID)

        x_plane = keep.tile([P, WINDOW], U8, name="x_plane", align_bytes=64)
        nc.gpsimd.memset(x_plane[:], 0)
        x_words = []
        for s in range(PASSES):
            words = keep.tile([P, WINDOW], I32, name=f"x_words{s}", align_bytes=64)
            nc.gpsimd.memset(words[:, T:], 0)
            x_words.append(words)
        windows = []
        for q in range(4):
            window = keep.tile([P, T], F32, name=f"window{q}")
            nc.gpsimd.memset(window[:], 0.0)
            windows.append(window)

        slot_words = [keep.tile([P, E * C], U32, name=f"slot_words{s}", align_bytes=64) for s in range(PASSES)]
        slot_plane = keep.tile([P, E * C], U8, name="slot_plane", align_bytes=64)
        sums = {}
        held = {}

        def lists(e):
            return offsets[:, e * (C // 16) : (e + 1) * (C // 16)]

        def load(view, columns):
            raw = stage.tile([P, PACK, columns], F32, name="raw", align_bytes=64)
            nc.sync.dma_start(raw[:], view)
            return raw

        def x_copy(s):
            raw = load(xT[s * K_PASS : (s + 1) * K_PASS, :].rearrange("(p j) t -> p j t", j=PACK), T)
            grouped = work.tile([P, T * PACK], BF16, name="grouped", bufs=6, align_bytes=64)
            src = raw[:].rearrange("p j (c i) -> p c j i", i=4)
            dst = grouped[:].rearrange("p (c i j) -> p c j i", i=4, j=PACK)
            nc.vector.tensor_copy(dst[:, :X_VECTOR], src[:, :X_VECTOR])
            nc.scalar.activation(dst[:, X_VECTOR:], src[:, X_VECTOR:], COPY)
            held["x", s] = grouped
            if s == 0:
                nc.sync.dma_start(offsets[:], offs)

        def x_finish(s):
            grouped = held["x", s]
            for lo, hi in ((0, 512), (512, T)):
                nc.vector.quantize_mx(
                    out=x_words[s][:, lo:hi].bitcast(FP8X4),
                    scales=x_plane[4 * s : P, lo:hi],
                    in_=grouped[:, lo * PACK : hi * PACK],
                )
            nc.vector.tensor_copy(slot_words[s][:], x_words[s][:].bitcast(U32).indirect(offsets[:]))
            if s == PASSES - 1:
                nc.vector.tensor_copy(slot_plane[:], x_plane[:].indirect(offsets[:]))

        def w_copy(key, view):
            raw = load(view.rearrange("(p j) c -> p j c", j=PACK), 512)
            grouped = work.tile([P, 512 * PACK], BF16, name="grouped", bufs=6, align_bytes=64)
            src = raw[:].rearrange("p j (m t) -> p m j t", t=4)
            dst = grouped[:].rearrange("p (t m j) -> p m j t", t=4, j=PACK)
            share = vector_share(key)
            if share:
                nc.vector.tensor_copy(dst[:, :share], src[:, :share])
            nc.scalar.copy(dst[:, share:], src[:, share:])
            held[key] = grouped

        def w_quantize(key):
            words = coded.tile([P, 512], U32, name="w_words", align_bytes=64)
            plane = coded.tile([P, 512], U8, name="w_plane", align_bytes=64)
            nc.vector.quantize_mx(out=words[:].bitcast(FP8X4), scales=plane[:], in_=held[key][:])
            return words, plane

        def first_layer(key):
            e, m, s = key
            words, plane = w_quantize(key)
            for t in range(4):
                if s == 0:
                    sums[e, m, t] = psum.tile([P, 512], F32, name=f"bank_{m}_{t}")
                cols = slice(t * P, (t + 1) * P)
                nc.tensor.matmul_mx(
                    out=sums[e, m, t][:, :C],
                    lhsT=words[:, cols].bitcast(FP8X4),
                    lhsT_scale=plane[:, cols],
                    rhs=slot_words[s][:, e * C : (e + 1) * C].bitcast(FP8X4),
                    rhs_scale=slot_plane[4 * s : P, e * C : (e + 1) * C],
                    start=(s == 0),
                    stop=(s == PASSES - 1),
                )
            if s < PASSES - 1:
                return
            if m == "a":
                sig = work.tile([P, 4, C], F32, name="sig", bufs=1)
                for t in range(4):
                    nc.scalar.activation(sig[:, t, :], sums[e, m, t][:, :C], SIGMOID)
                held["sig", e] = sig
            else:
                hidden = work.tile([P, 4, C], BF16, name="hidden", bufs=1)
                for t in range(4):
                    nc.vector.tensor_tensor(hidden[:, t, :], held["sig", e][:, t, :], sums[e, m, t][:, :C], MULT)
                h_grouped = work.tile([P, C * PACK], BF16, name="h_grouped", bufs=1, align_bytes=64)
                nc.vector.tensor_copy(
                    h_grouped[:].rearrange("p (c i t) -> p c t i", i=4, t=4),
                    hidden[:].rearrange("p t (c i) -> p c t i", i=4),
                )
                h_words = work.tile([P, C], U32, name="h_words", bufs=2, align_bytes=64)
                h_plane = work.tile([P, C], U8, name="h_plane", bufs=2, align_bytes=64)
                nc.vector.quantize_mx(out=h_words[:].bitcast(FP8X4), scales=h_plane[:], in_=h_grouped[:])
                held["h", e] = h_words, h_plane

        def second_layer(e, q, bank, half):
            words, plane = held["w2q", e]
            h_words, h_plane = held["h", e]
            cols = slice(q * P, (q + 1) * P)
            nc.tensor.matmul_mx(
                out=bank[:, half * C : (half + 1) * C],
                lhsT=words[:, cols].bitcast(FP8X4),
                lhsT_scale=plane[:, cols],
                rhs=h_words[:].bitcast(FP8X4),
                rhs_scale=h_plane[:],
                start=True,
                stop=True,
            )

        def pair(e, u):
            bank = psum.tile([P, 512], F32, name=f"bank_b_{u}")
            for half in range(2):
                second_layer(e, 2 * u + half, bank, half)
            y = work.tile([P, 2, C], F32, name="y", bufs=2)
            nc.scalar.copy(y[:].rearrange("p a c -> p (a c)"), bank[:])
            held["y", u] = y

        def scatter(e, q):
            nc.vector.tensor_tensor(windows[q][:].indirect(lists(e)), held["y", q // 2][:, q % 2, :], held["gate", e][:, q, :], MULT)

        def rows(dram):
            return dram.rearrange("(p q) t -> p q t", q=4)

        plan = [("x", s) for s in range(PASSES)]
        for e in range(E):
            plan += [(e, "a", s) for s in range(PASSES)] + [(e, "b", s) for s in range(PASSES)] + [("w2", e)]

        def copy_step(key):
            if key[0] == "x":
                x_copy(key[1])
            elif key[0] == "w2":
                e = key[1]
                w_copy(key, w2[e])
                held["gate", e] = load(rows(gate)[:, :, e * C : (e + 1) * C], C)
            else:
                e, m, s = key
                w_copy(key, (w1 if m == "a" else w3)[e, s * K_PASS : (s + 1) * K_PASS, :])

        def finish_step(key):
            if key[0] == "x":
                x_finish(key[1])
            elif key[0] == "w2":
                held["w2q", key[1]] = w_quantize(key)
            else:
                first_layer(key)
                e, m, s = key
                if e == 1:
                    i = s if m == "a" else 4 + s
                    if i < 2:
                        pair(0, i)
                    if i in (1, 3, 5, 7):
                        scatter(0, i // 2)

        for i, key in enumerate(plan):
            copy_step(key)
            if i > 0:
                finish_step(plan[i - 1])
        finish_step(plan[-1])

        residual = load(rows(xr), T)
        scaled = []

        def finish(q):
            nc.vector.tensor_copy(windows[q][:].indirect(lists(1)), scaled[q][:])
            result = work.tile([P, T], F32, name="result")
            engine = nc.gpsimd if q < 3 else nc.vector
            engine.tensor_tensor(result[:], windows[q][:], residual[:, q, :], ADD)
            nc.sync.dma_start(rows(out)[:, q, :], result[:])

        for q in range(4):
            bank = psum.tile([P, 512], F32, name=f"bank_a_{q}")
            second_layer(1, q, bank, 0)
            z = work.tile([P, C], F32, name="z")
            nc.vector.tensor_tensor(z[:], bank[:, :C], held["gate", 1][:, q, :], MULT)
            scaled.append(z)
            if q > 0:
                finish(q - 1)
        finish(3)
